import numpy as np, ml_dtypes
CORES = [0,1,2,3]
N = 4
def setup_inputs(rng):
    return {"x": rng.standard_normal((N, 128, 128), dtype=np.float32).astype(ml_dtypes.bfloat16)}
def reference(x):
    s = x.max(axis=0)
    b = 128 // N
    return {"y": np.stack([s[:, r * b:(r + 1) * b] for r in range(N)])}

@@ -1,0 +1,60 @@
+from concourse.bass import DstId, RemoteDMATransfer
+
+N = 4
+B = 128 // N
+
+SCRATCH = {
+    "xs": ("sbuf", [128, 128], "bfloat16"),
+    "land": ("sbuf", [128, (N - 1) * B], "bfloat16"),
+    "res": ("sbuf", [128, B], "bfloat16"),
+}
+SEMAPHORES = ["loaded", "sent", "arrived", "result", "stored"]
+
+GATHER_ENGINES = 4
+FOLD_ENGINES = 16
+
+
+def rank_program(g, core, T, topo):
+    r = T.rank_of(core)
+    if r is None:
+        return
+
+    def dst_id(rank):
+        rid, pid, _se = topo.addr(T.cores[rank])
+        return DstId(rid=rid, pnc=pid)
+
+    def block(j):
+        return T.xs[:, j * B:(j + 1) * B]
+
+    g.sync.dma_start(T.xs[:], T.x[:]).then_inc(T.sem.loaded, 16)
+    g.wait_ge(T.sem.loaded, 16)
+
+    transfers = []
+    for k in range(1, N):
+        p = (r + k) % N
+        slot = (r - p) % N - 1
+        transfers.append(RemoteDMATransfer(
+            dst_ids=[dst_id(p)],
+            dma_engine_mask=((1 << GATHER_ENGINES) - 1) << (GATHER_ENGINES * (k - 1)),
+            remote_sem=T.sem.arrived,
+            src=block(p ^ 1),
+            dst=T.land[:, slot * B:(slot + 1) * B],
+        ))
+    g.remote_dma_fused(transfers, local_sem=T.sem.sent)
+
+    partner = r ^ 1
+    g.wait_ge(T.sem.arrived, (N - 1) * GATHER_ENGINES)
+    g.remote_dma_fused([RemoteDMATransfer(
+        dst_ids=[dst_id(partner)],
+        dma_engine_mask=(1 << FOLD_ENGINES) - 1,
+        remote_sem=T.sem.result,
+        srcs=[block(partner)] + [T.land[:, s * B:(s + 1) * B] for s in range(N - 1)],
+        dsts=[T.res[:]],
+        alu_op=2,
+    )], local_sem=T.sem.sent)
+
+    g.sync.wait_ge(T.sem.result, FOLD_ENGINES)
+    g.sync.dma_start(T.y[:], T.res[:]).then_inc(T.sem.stored, 16)
+
+    g.wait_ge(T.sem.sent, (N - 1) * GATHER_ENGINES + FOLD_ENGINES)
+    g.wait_ge(T.sem.stored, 16)

@@ -4,11 +4,11 @@ N = 4
 B = 128 // N
 
 SCRATCH = {
-    "xs": ("sbuf", [128, 128], "bfloat16"),
-    "land": ("sbuf", [128, (N - 1) * B], "bfloat16"),
-    "res": ("sbuf", [128, B], "bfloat16"),
+    "blk": ("dram", [N, 128, B], "bfloat16"),
+    "land": ("dram", [N - 1, 128, B], "bfloat16"),
+    "res": ("dram", [128, B], "bfloat16"),
 }
-SEMAPHORES = ["loaded", "sent", "arrived", "result", "stored"]
+SEMAPHORES = ["loaded", "own", "sent", "arrived", "result", "stored"]
 
 GATHER_ENGINES = 4
 FOLD_ENGINES = 16
@@ -23,32 +23,35 @@ def rank_program(g, core, T, topo):
         rid, pid, _se = topo.addr(T.cores[rank])
         return DstId(rid=rid, pnc=pid)
 
-    def block(j):
-        return T.xs[:, j * B:(j + 1) * B]
+    partner = r ^ 1
+    peers = [(r + k) % N for k in range(1, N)]
+    outgoing = [p ^ 1 for p in peers]
 
-    g.sync.dma_start(T.xs[:], T.x[:]).then_inc(T.sem.loaded, 16)
-    g.wait_ge(T.sem.loaded, 16)
+    queues = [g.sync, g.scalar, g.sync]
+    for q, j in zip(queues, outgoing):
+        q.dma_start(T.blk[j], T.x[:, j * B:(j + 1) * B]).then_inc(T.sem.loaded, 16)
+    g.scalar.dma_start(T.blk[partner], T.x[:, partner * B:(partner + 1) * B]).then_inc(T.sem.own, 16)
 
+    g.wait_ge(T.sem.loaded, 16 * (N - 1))
     transfers = []
-    for k in range(1, N):
-        p = (r + k) % N
+    for k, p in enumerate(peers):
         slot = (r - p) % N - 1
         transfers.append(RemoteDMATransfer(
             dst_ids=[dst_id(p)],
-            dma_engine_mask=((1 << GATHER_ENGINES) - 1) << (GATHER_ENGINES * (k - 1)),
+            dma_engine_mask=((1 << GATHER_ENGINES) - 1) << (GATHER_ENGINES * k),
             remote_sem=T.sem.arrived,
-            src=block(p ^ 1),
-            dst=T.land[:, slot * B:(slot + 1) * B],
+            src=T.blk[p ^ 1],
+            dst=T.land[slot],
         ))
     g.remote_dma_fused(transfers, local_sem=T.sem.sent)
 
-    partner = r ^ 1
+    g.wait_ge(T.sem.own, 16)
     g.wait_ge(T.sem.arrived, (N - 1) * GATHER_ENGINES)
     g.remote_dma_fused([RemoteDMATransfer(
         dst_ids=[dst_id(partner)],
         dma_engine_mask=(1 << FOLD_ENGINES) - 1,
         remote_sem=T.sem.result,
-        srcs=[block(partner)] + [T.land[:, s * B:(s + 1) * B] for s in range(N - 1)],
+        srcs=[T.blk[partner]] + [T.land[s] for s in range(N - 1)],
         dsts=[T.res[:]],
         alu_op=2,
     )], local_sem=T.sem.sent)

from concourse.bass import DstId, RemoteDMATransfer

N = 4
B = 128 // N

SCRATCH = {
    "blk": ("dram", [N, 128, B], "bfloat16"),
    "land": ("dram", [N - 1, 128, B], "bfloat16"),
    "res": ("dram", [128, B], "bfloat16"),
}
SEMAPHORES = ["loaded", "own", "sent", "arrived", "result", "stored"]

GATHER_ENGINES = 4
FOLD_ENGINES = 16


def rank_program(g, core, T, topo):
    r = T.rank_of(core)
    if r is None:
        return

    def dst_id(rank):
        rid, pid, _se = topo.addr(T.cores[rank])
        return DstId(rid=rid, pnc=pid)

    partner = r ^ 1
    peers = [(r + k) % N for k in range(1, N)]
    outgoing = [p ^ 1 for p in peers]

    queues = [g.sync, g.scalar, g.sync]
    for q, j in zip(queues, outgoing):
        q.dma_start(T.blk[j], T.x[:, j * B:(j + 1) * B]).then_inc(T.sem.loaded, 16)
    g.scalar.dma_start(T.blk[partner], T.x[:, partner * B:(partner + 1) * B]).then_inc(T.sem.own, 16)

    g.wait_ge(T.sem.loaded, 16 * (N - 1))
    transfers = []
    for k, p in enumerate(peers):
        slot = (r - p) % N - 1
        transfers.append(RemoteDMATransfer(
            dst_ids=[dst_id(p)],
            dma_engine_mask=((1 << GATHER_ENGINES) - 1) << (GATHER_ENGINES * k),
            remote_sem=T.sem.arrived,
            src=T.blk[p ^ 1],
            dst=T.land[slot],
        ))
    g.remote_dma_fused(transfers, local_sem=T.sem.sent)

    g.wait_ge(T.sem.own, 16)
    g.wait_ge(T.sem.arrived, (N - 1) * GATHER_ENGINES)
    g.remote_dma_fused([RemoteDMATransfer(
        dst_ids=[dst_id(partner)],
        dma_engine_mask=(1 << FOLD_ENGINES) - 1,
        remote_sem=T.sem.result,
        srcs=[T.blk[partner]] + [T.land[s] for s in range(N - 1)],
        dsts=[T.res[:]],
        alu_op=2,
    )], local_sem=T.sem.sent)

    g.sync.wait_ge(T.sem.result, FOLD_ENGINES)
    g.sync.dma_start(T.y[:], T.res[:]).then_inc(T.sem.stored, 16)

    g.wait_ge(T.sem.sent, (N - 1) * GATHER_ENGINES + FOLD_ENGINES)
    g.wait_ge(T.sem.stored, 16)
